import numpy as np
import ml_dtypes


def mxq(x, axis, fmt="e4m3"):
    dtype, down = {"e4m3": (ml_dtypes.float8_e4m3fn, 7), "e5m2": (ml_dtypes.float8_e5m2, 14)}[fmt]
    v = np.moveaxis(np.asarray(x, np.float32).astype(ml_dtypes.bfloat16).astype(np.float64), axis, -1)
    blocks = v.reshape(v.shape[:-1] + (-1, 32))
    amax = np.abs(blocks).max(-1, keepdims=True)
    byte = np.maximum(np.where(amax > 0, np.frexp(amax)[1] - 1 + 127, 0) - down, 1)
    scale = np.exp2(byte - 127.0)
    codes = (blocks / scale).astype(np.float32).astype(dtype).astype(np.float64)
    return np.moveaxis((codes * scale).reshape(v.shape), -1, axis)


WIDE = False


def mx_kscale(k):
    if not WIDE:
        return np.ones(k)
    levels = np.array([10, -10, 5, -5, 0])
    if k % 512:
        return np.exp2(np.random.permutation(np.resize(levels, k // 32))).repeat(32)
    a = np.empty((k // 512, 16))
    for p in range(k // 512):
        a[p, :8] = np.random.permutation(np.resize(levels, 8))
        for g in range(8):
            far = levels[np.abs(levels - a[p, g]) >= 10]
            a[p, g + 8] = far[np.random.randint(len(far))]
    return np.exp2(a.ravel()).repeat(32)


def f64(x):
    return np.asarray(x).astype(np.float64)


def striped(idx):
    return np.tile(idx.reshape(-1, 16).T, (8, 1)).astype(np.uint16)


def unstriped(offs):
    return offs[:16].T.reshape(-1).astype(np.int64)


def d_relu2(v):
    return 2.0 * np.maximum(v, 0.0)


K, T, E, C, H, N = 512, 768, 12, 128, 512, 512


def by_expert(wq, xq):
    return np.concatenate([wq[e].T @ xq[:, e * C:(e + 1) * C] for e in range(E)], axis=1)


def setup_inputs():
    n = np.random.standard_normal
    s = mx_kscale(N)[:, None]
    u = mx_kscale(H)
    first = np.random.permutation(np.repeat(np.arange(E), T // E))
    second = (first + 1 + np.random.permutation(np.repeat(np.arange(E - 1), -(-T // (E - 1)))[:T])) % E
    while np.bincount(second, minlength=E).max() != T // E:
        load = np.bincount(second, minlength=E); hi, lo = int(load.argmax()), int(load.argmin())
        t = np.flatnonzero((second == hi) & (first != lo))[0]; second[t] = lo
    slot_token = np.empty(E * C, np.int64); pos = np.empty((2, T), np.int64); fill = np.zeros(E, np.int64)
    place = np.stack([np.random.permutation(C) for _ in range(E)])
    for r, deal in enumerate((first, second)):
        for t in np.random.permutation(T):
            e = deal[t]; j = e * C + place[e, fill[e]]; fill[e] += 1; slot_token[j] = t; pos[r, t] = j
    g = np.random.uniform(0.2, 0.8, T)
    w_slot = np.empty(E * C); w_slot[pos[0]] = g; w_slot[pos[1]] = 1.0 - g
    return {
        "dyT": (n((N, T)) * s).astype(np.float32),
        "a": n((H, E * C)).astype(np.float32),
        "w2": (n((E, N, H)) / np.sqrt(N) / s[None] * u[None, None, :]).astype(np.float32),
        "w1": (n((E, H, K)) / np.sqrt(H) / u[None, :, None]).astype(np.float32),
        "gate": np.tile(w_slot, (N, 1)).astype(np.float32),
        "offs": striped(slot_token),
        "pos1": striped(pos[0]),
        "pos2": striped(pos[1]),
    }


def reference(dyT, a, w2, w1, gate, offs, pos1, pos2):
    idx = unstriped(offs)
    gq = mxq(f64(gate) * f64(dyT)[:, idx], 0, "e4m3")
    dh = by_expert(mxq(f64(w2), 1, "e4m3"), gq)
    da = dh * d_relu2(f64(a))
    dx = by_expert(mxq(f64(w1), 1, "e4m3"), mxq(da, 0, "e4m3"))
    return dx[:, unstriped(pos1)] + dx[:, unstriped(pos2)]

@@ -1,0 +1,274 @@
+from contextlib import ExitStack
+
+import concourse.mybir as mybir
+
+K, T, E, C, H, N = 512, 768, 12, 128, 512, 512
+S = E * C
+
+F32 = mybir.dt.float32
+BF16 = mybir.dt.bfloat16
+U32 = mybir.dt.uint32
+U16 = mybir.dt.uint16
+U8 = mybir.dt.uint8
+FP8X4 = mybir.dt.float8_e4m3fn_x4
+MULT = mybir.AluOpType.mult
+ADD = mybir.AluOpType.add
+MAX = mybir.AluOpType.max
+COPY = mybir.ActivationFunctionType.Copy
+
+FLOPS = 2 * 2 * S * N * H
+BYTES = 4 * (N * T + H * S + 2 * E * N * H + S + K * T) + 2 * 128 * (S + 2 * T) // 16
+
+P = 128
+PACK = 4
+GROUPS = (256, 256, 512, 512)
+W1_WIDTHS = (256, 256)
+A_W = 256
+RING = 9
+
+
+def tile_moe_bdx_mlp_relu2_kernel(tc, dyT, a, w2, w1, gate, offs, pos1, pos2, out):
+    nc = tc.nc
+    with ExitStack() as ctx:
+        held = ctx.enter_context(tc.tile_pool(name="held", bufs=1))
+        work = ctx.enter_context(tc.tile_pool(name="work", bufs=2))
+        psum = ctx.enter_context(tc.psum_pool(name="psum", bufs=4))
+
+        offs_t = held.tile([P, S // 16], U16)
+        nc.sync.dma_start(offs_t[:], offs)
+
+        group_start = [sum(GROUPS[:g]) for g in range(len(GROUPS))]
+        gate_t = []
+        for g, n in enumerate(GROUPS):
+            gt = held.tile([P, n], F32, name=f"gate{g}")
+            gate_t.append(gt)
+
+        def load_gate(g):
+            s0 = group_start[g]
+            nc.sync.dma_start(gate_t[g][:], gate[0:P, s0 : s0 + GROUPS[g]])
+
+        load_gate(0)
+        dy_rows = dyT.rearrange("(p j) t -> p j t", j=PACK)
+        dy = []
+        for j in range(PACK):
+            d = held.tile([P, T], F32, name=f"dy{j}")
+            nc.sync.dma_start(d[:], dy_rows[:, j, :])
+            dy.append(d)
+
+        a_rows = a.rearrange("(p j) s -> p j s", j=PACK)
+        g_codes = []
+        g_scales = []
+        for g, n in enumerate(GROUPS):
+            gc = held.tile([P, n], U32, name=f"gc{g}", align_bytes=64)
+            gs = held.tile([P, n], U8, name=f"gs{g}", align_bytes=64)
+            g_codes.append(gc)
+            g_scales.append(gs)
+        pos1_t = held.tile([P, T // 16], U16)
+        pos2_t = held.tile([P, T // 16], U16)
+
+        raw = {}
+
+        def load_a(c):
+            at = work.tile([P, PACK, A_W], F32, name="a_t", bufs=3)
+            nc.sync.dma_start(at[:], a_rows[:, :, c * A_W : (c + 1) * A_W])
+            raw["a", c] = at
+
+        def load_w2(e):
+            wr = work.tile([P, PACK * H], F32, name="raw", bufs=RING)
+            wr = wr[:].rearrange("p (j i) -> p j i", j=PACK)
+            rows = w2[e].rearrange("(p j) i -> p j i", j=PACK)
+            for j in range(0, PACK, 2):
+                nc.sync.dma_start(wr[:, j : j + 2, :], rows[:, j : j + 2, :])
+            raw["w2", e] = wr
+
+        def load_w1(k0, width, e):
+            wr = work.tile([P, PACK * H], F32, name="raw", bufs=RING)
+            wr = wr[:].rearrange("p (s j k) -> p s j k", j=PACK, k=width)
+            for s in range(H // width):
+                rows = w1[e + s].rearrange("(p j) k -> p j k", j=PACK)
+                nc.sync.dma_start(wr[:, s], rows[:, :, k0 : k0 + width])
+            raw["w1", k0, e] = wr
+
+        def load_pos():
+            nc.sync.dma_start(pos1_t[:], pos1)
+            nc.sync.dma_start(pos2_t[:], pos2)
+
+        loads = []
+        for e in range(E):
+            loads.append(lambda e=e: load_w2(e))
+            if e * C % A_W == 0:
+                loads.append(lambda e=e: load_a(e * C // A_W))
+            for g in range(1, len(GROUPS)):
+                if e == max(0, group_start[g] // C - 2):
+                    loads.append(lambda g=g: load_gate(g))
+            if e == 8:
+                loads.append(load_pos)
+        k0 = 0
+        for width in W1_WIDTHS:
+            for e in range(0, E, H // width):
+                loads.append(lambda k0=k0, width=width, e=e: load_w1(k0, width, e))
+            k0 += width
+
+        def advance(n):
+            for _ in range(n):
+                if loads:
+                    loads.pop(0)()
+
+        def make_g(g):
+            n = GROUPS[g]
+            s0 = group_start[g]
+            g32 = work.tile([P, PACK, 512], F32, name="g32")
+            for j in range(PACK):
+                nc.vector.tensor_tensor(
+                    g32[:, j, 0:n],
+                    dy[j][:].indirect(offs_t[:, s0 // 16 : (s0 + n) // 16]),
+                    gate_t[g][:],
+                    MULT,
+                )
+            gb = work.tile([P, 512 * PACK], BF16, name="gb", align_bytes=64)
+            nc.scalar.copy(
+                gb[:, 0 : n * PACK].rearrange("p (c i j) -> p c j i", i=4, j=PACK),
+                g32[:, :, 0:n].rearrange("p j (c i) -> p c j i", i=4),
+            )
+            nc.vector.quantize_mx(out=g_codes[g][:].bitcast(FP8X4), scales=g_scales[g][:], in_=gb[:, 0 : n * PACK])
+
+        w2_q = {}
+
+        def make_w2(e):
+            while ("w2", e) not in raw:
+                advance(1)
+            wr = raw.pop(("w2", e))
+            wb = work.tile([P, H * PACK], BF16, name="wb", bufs=3, align_bytes=64)
+            dst = wb[:].rearrange("p (t m j) -> p m j t", t=PACK, j=PACK)
+            src = wr.rearrange("p j (m t) -> p m j t", t=PACK)
+            cut = 64 if e % 4 == 3 else 0
+            if cut:
+                nc.vector.tensor_copy(dst[:, 0:cut], src[:, 0:cut])
+            nc.scalar.copy(dst[:, cut:P], src[:, cut:P])
+            wc = work.tile([P, H], U32, name="wc", bufs=3, align_bytes=64)
+            ws = work.tile([P, H], U8, name="ws", bufs=3, align_bytes=64)
+            nc.vector.quantize_mx(out=wc[:].bitcast(FP8X4), scales=ws[:], in_=wb[:])
+            w2_q[e] = (wc, ws)
+
+        da_q = []
+        pair = {}
+
+        def layer2(e):
+            g = max(i for i in range(len(GROUPS)) if group_start[i] <= e * C)
+            cols = slice(e * C - group_start[g], e * C - group_start[g] + C)
+            wc, ws = w2_q.pop(e)
+            dh = psum.tile([P, PACK, C], F32, name="dh", bufs=3)
+            for t in range(PACK):
+                nc.tensor.matmul_mx(
+                    out=dh[:, t, :],
+                    lhsT=wc[:, t * P : (t + 1) * P].bitcast(FP8X4),
+                    lhsT_scale=ws[:, t * P : (t + 1) * P],
+                    rhs=g_codes[g][:, cols].bitcast(FP8X4),
+                    rhs_scale=g_scales[g][:, cols],
+                    start=True,
+                    stop=True,
+                )
+            if e % 2 == 0:
+                db = work.tile([P, 2 * C * PACK], BF16, name="db", align_bytes=64)
+                pair["db"] = db
+            db = pair["db"]
+            half = e % 2 * C
+            a0 = e * C % A_W
+            nc.vector.scalar_tensor_tensor(
+                db[:, half * PACK : (half + C) * PACK].rearrange("p (n t) -> p n t", t=PACK),
+                raw["a", e * C // A_W][:, :, a0 : a0 + C].rearrange("p t n -> p n t"),
+                0.0,
+                dh[:].rearrange("p t n -> p n t"),
+                MAX,
+                MULT,
+            )
+            if e % 2 == 1:
+                dc = held.tile([P, 2 * C], U32, name=f"dc{e}", align_bytes=64)
+                ds = held.tile([P, 2 * C], U8, name=f"ds{e}", align_bytes=64)
+                nc.vector.quantize_mx(out=dc[:].bitcast(FP8X4), scales=ds[:], in_=db[:])
+                da_q.append((dc, ds))
+
+        advance(6)
+        make_g(0)
+        make_w2(0)
+        first_of_group = {group_start[g] // C: g for g in range(1, len(GROUPS))}
+        for e in range(E):
+            advance(2)
+            if e + 1 in first_of_group:
+                make_g(first_of_group[e + 1])
+            if e + 1 < E:
+                make_w2(e + 1)
+            layer2(e)
+
+        dx = []
+        for kt in range(K // P):
+            d = held.tile([P, S], F32, name=f"dx{kt}")
+            dx.append(d)
+
+        def combine(kt, queue):
+            r1 = work.tile([P, T], F32, name="r1")
+            r2 = work.tile([P, T], F32, name="r2")
+            res = work.tile([P, T], F32, name="res")
+
+            def first():
+                nc.vector.tensor_copy(r1[:], dx[kt][:].indirect(pos1_t[:]))
+
+            def second():
+                nc.vector.tensor_copy(r2[:], dx[kt][:].indirect(pos2_t[:]))
+
+            def finish():
+                nc.gpsimd.tensor_tensor(res[:], r1[:], r2[:], ADD)
+                queue.dma_start(out[kt * P : (kt + 1) * P, :], res[:])
+
+            return [first, second, finish]
+
+        k0 = 0
+        pending = []
+        for width in W1_WIDTHS:
+            n = H // width
+            for e in range(0, E, n):
+                while ("w1", k0, e) not in raw:
+                    advance(1)
+                advance(1)
+                wr = raw.pop(("w1", k0, e))
+                wb = work.tile([P, H * PACK], BF16, name="wb", bufs=3, align_bytes=64)
+                dst = wb[:].rearrange("p (s c i j) -> p s c j i", s=n, i=4, j=PACK)
+                src = wr.rearrange("p s j (c i) -> p s c j i", i=4)
+                for s in range(n):
+                    if s % 2 == 1:
+                        nc.vector.tensor_copy(dst[:, s], src[:, s])
+                    else:
+                        nc.scalar.copy(dst[:, s], src[:, s])
+                wc = work.tile([P, H], U32, name="wc", bufs=3, align_bytes=64)
+                ws = work.tile([P, H], U8, name="ws", bufs=3, align_bytes=64)
+                nc.vector.quantize_mx(out=wc[:].bitcast(FP8X4), scales=ws[:], in_=wb[:])
+                bank = psum.tile([P, width // P, n, C], F32, name="bank", bufs=4)
+                for s in range(n):
+                    dc, ds = da_q[(e + s) // 2]
+                    cols = slice((e + s) % 2 * C, (e + s) % 2 * C + C)
+                    for b in range(width // P):
+                        w0 = s * width + b * P
+                        nc.tensor.matmul_mx(
+                            out=bank[:, b, s, :],
+                            lhsT=wc[:, w0 : w0 + P].bitcast(FP8X4),
+                            lhsT_scale=ws[:, w0 : w0 + P],
+                            rhs=dc[:, cols].bitcast(FP8X4),
+                            rhs_scale=ds[:, cols],
+                            start=True,
+                            stop=True,
+                        )
+                for b in range(width // P):
+                    nc.scalar.activation(
+                        dx[k0 // P + b][:, e * C : (e + n) * C].rearrange("p (s c) -> p s c", c=C),
+                        bank[:, b],
+                        COPY,
+                        scale=2.0,
+                    )
+                if pending:
+                    pending.pop(0)()
+            last = k0 + width == K
+            for b in range(width // P):
+                pending += combine(k0 // P + b, nc.sync if last else nc.gpsimd)
+            k0 += width
+        for step in pending:
+            step()

@@ -21,10 +21,13 @@ BYTES = 4 * (N * T + H * S + 2 * E * N * H + S + K * T) + 2 * 128 * (S + 2 * T) 
 
 P = 128
 PACK = 4
-GROUPS = (256, 256, 512, 512)
-W1_WIDTHS = (256, 256)
+G_W = 512
 A_W = 256
-RING = 9
+GROUPS = S // G_W
+W2_V = (0,) * 8 + (32,) * 4
+W1_V = (48,) * 6 + (32,) * 6
+QUAD = 4
+UNITS = 2 * E
 
 
 def tile_moe_bdx_mlp_relu2_kernel(tc, dyT, a, w2, w1, gate, offs, pos1, pos2, out):
@@ -35,17 +38,25 @@ def tile_moe_bdx_mlp_relu2_kernel(tc, dyT, a, w2, w1, gate, offs, pos1, pos2, ou
         psum = ctx.enter_context(tc.psum_pool(name="psum", bufs=4))
 
         offs_t = held.tile([P, S // 16], U16)
+        pos1_t = held.tile([P, T // 16], U16)
+        pos2_t = held.tile([P, T // 16], U16)
+        gate_t = []
+        g_q = []
+        for g in range(GROUPS):
+            gt = held.tile([P, G_W], F32, name=f"gate{g}")
+            gate_t.append(gt)
+            gc = held.tile([P, G_W], U32, name=f"gc{g}", align_bytes=64)
+            gs = held.tile([P, G_W], U8, name=f"gs{g}", align_bytes=64)
+            g_q.append((gc, gs))
+        dx = []
+        for q in range(K // P):
+            d = held.tile([P, S], F32, name=f"dx{q}")
+            dx.append(d)
+
         nc.sync.dma_start(offs_t[:], offs)
 
-        group_start = [sum(GROUPS[:g]) for g in range(len(GROUPS))]
-        gate_t = []
-        for g, n in enumerate(GROUPS):
-            gt = held.tile([P, n], F32, name=f"gate{g}")
-            gate_t.append(gt)
-
         def load_gate(g):
-            s0 = group_start[g]
-            nc.sync.dma_start(gate_t[g][:], gate[0:P, s0 : s0 + GROUPS[g]])
+            nc.sync.dma_start(gate_t[g][:], gate[0:P, g * G_W : (g + 1) * G_W])
 
         load_gate(0)
         dy_rows = dyT.rearrange("(p j) t -> p j t", j=PACK)
@@ -56,219 +67,231 @@ def tile_moe_bdx_mlp_relu2_kernel(tc, dyT, a, w2, w1, gate, offs, pos1, pos2, ou
             dy.append(d)
 
         a_rows = a.rearrange("(p j) s -> p j s", j=PACK)
-        g_codes = []
-        g_scales = []
-        for g, n in enumerate(GROUPS):
-            gc = held.tile([P, n], U32, name=f"gc{g}", align_bytes=64)
-            gs = held.tile([P, n], U8, name=f"gs{g}", align_bytes=64)
-            g_codes.append(gc)
-            g_scales.append(gs)
-        pos1_t = held.tile([P, T // 16], U16)
-        pos2_t = held.tile([P, T // 16], U16)
-
         raw = {}
+        a_t = {}
 
-        def load_a(c):
+        def load_a(g):
             at = work.tile([P, PACK, A_W], F32, name="a_t", bufs=3)
-            nc.sync.dma_start(at[:], a_rows[:, :, c * A_W : (c + 1) * A_W])
-            raw["a", c] = at
+            nc.sync.dma_start(at[:], a_rows[:, :, g * A_W : (g + 1) * A_W])
+            a_t[g] = at
 
-        def load_w2(e):
-            wr = work.tile([P, PACK * H], F32, name="raw", bufs=RING)
-            wr = wr[:].rearrange("p (j i) -> p j i", j=PACK)
-            rows = w2[e].rearrange("(p j) i -> p j i", j=PACK)
-            for j in range(0, PACK, 2):
-                nc.sync.dma_start(wr[:, j : j + 2, :], rows[:, j : j + 2, :])
-            raw["w2", e] = wr
-
-        def load_w1(k0, width, e):
-            wr = work.tile([P, PACK * H], F32, name="raw", bufs=RING)
-            wr = wr[:].rearrange("p (s j k) -> p s j k", j=PACK, k=width)
-            for s in range(H // width):
-                rows = w1[e + s].rearrange("(p j) k -> p j k", j=PACK)
-                nc.sync.dma_start(wr[:, s], rows[:, :, k0 : k0 + width])
-            raw["w1", k0, e] = wr
+        def load_unit(u):
+            wr = work.tile([P, PACK, H], F32, name="raw", bufs=9)
+            if u < E:
+                rows = w2[u].rearrange("(p j) i -> p j i", j=PACK)
+                for j in range(0, PACK, 2):
+                    nc.sync.dma_start(wr[:, j : j + 2, :], rows[:, j : j + 2, :])
+            else:
+                q, quad = divmod(u - E, E // QUAD)
+                for s in range(QUAD):
+                    rows = w1[quad * QUAD + s].rearrange("(p j) k -> p j k", j=PACK)
+                    nc.sync.dma_start(wr[:, :, s * P : (s + 1) * P], rows[:, :, q * P : (q + 1) * P])
+            raw[u] = wr
 
         def load_pos():
             nc.sync.dma_start(pos1_t[:], pos1)
             nc.sync.dma_start(pos2_t[:], pos2)
 
         loads = []
-        for e in range(E):
-            loads.append(lambda e=e: load_w2(e))
-            if e * C % A_W == 0:
-                loads.append(lambda e=e: load_a(e * C // A_W))
-            for g in range(1, len(GROUPS)):
-                if e == max(0, group_start[g] // C - 2):
-                    loads.append(lambda g=g: load_gate(g))
-            if e == 8:
+        for u in range(UNITS):
+            loads.append(lambda u=u: load_unit(u))
+            if u < E and u % 2 == 0:
+                loads.append(lambda u=u: load_a(u // 2))
+                if u in (0, 4):
+                    loads.append(lambda u=u: load_gate(u // 4 + 1))
+            if u == 10:
                 loads.append(load_pos)
-        k0 = 0
-        for width in W1_WIDTHS:
-            for e in range(0, E, H // width):
-                loads.append(lambda k0=k0, width=width, e=e: load_w1(k0, width, e))
-            k0 += width
 
         def advance(n):
             for _ in range(n):
                 if loads:
                     loads.pop(0)()
 
-        def make_g(g):
-            n = GROUPS[g]
-            s0 = group_start[g]
-            g32 = work.tile([P, PACK, 512], F32, name="g32")
-            for j in range(PACK):
-                nc.vector.tensor_tensor(
-                    g32[:, j, 0:n],
-                    dy[j][:].indirect(offs_t[:, s0 // 16 : (s0 + n) // 16]),
-                    gate_t[g][:],
-                    MULT,
-                )
-            gb = work.tile([P, 512 * PACK], BF16, name="gb", align_bytes=64)
-            nc.scalar.copy(
-                gb[:, 0 : n * PACK].rearrange("p (c i j) -> p c j i", i=4, j=PACK),
-                g32[:, :, 0:n].rearrange("p j (c i) -> p c j i", i=4),
+        g32 = {}
+        gb = {}
+
+        def gather(g, j):
+            if j == 0:
+                gt = work.tile([P, PACK, G_W], F32, name="g32")
+                g32[g] = gt
+            lst = offs_t[:, g * G_W // 16 : (g + 1) * G_W // 16]
+            nc.vector.tensor_tensor(g32[g][:, j, :], dy[j][:].indirect(lst), gate_t[g][:], MULT)
+
+        def interleave(dst, src, c0, c1, copy):
+            copy(
+                dst[:].rearrange("p (c i j) -> p c j i", i=4, j=PACK)[:, c0:c1],
+                src[:].rearrange("p j (c i) -> p c j i", i=4)[:, c0:c1],
             )
-            nc.vector.quantize_mx(out=g_codes[g][:].bitcast(FP8X4), scales=g_scales[g][:], in_=gb[:, 0 : n * PACK])
 
-        w2_q = {}
+        def pack_g(g):
+            gt = work.tile([P, G_W * PACK], BF16, name="gb", align_bytes=64)
+            interleave(gt, g32.pop(g), 0, G_W // 4, nc.scalar.copy)
+            gb[g] = gt
 
-        def make_w2(e):
-            while ("w2", e) not in raw:
+        def quant_g(g):
+            nc.vector.quantize_mx(out=g_q[g][0][:].bitcast(FP8X4), scales=g_q[g][1][:], in_=gb.pop(g)[:])
+
+        wb = {}
+        w_q = {}
+
+        def pack(u, c0, c1, copy):
+            if u < E:
+                copy(
+                    wb[u][:].rearrange("p (t m j) -> p m j t", t=PACK, j=PACK)[:, c0:c1],
+                    raw[u][:].rearrange("p j (m t) -> p m j t", t=PACK)[:, c0:c1],
+                )
+            else:
+                interleave(wb[u], raw[u], c0, c1, copy)
+
+        def cut(u):
+            return W2_V[u] if u < E else W1_V[u - E]
+
+        def pack_scalar(u):
+            while u not in raw:
                 advance(1)
-            wr = raw.pop(("w2", e))
-            wb = work.tile([P, H * PACK], BF16, name="wb", bufs=3, align_bytes=64)
-            dst = wb[:].rearrange("p (t m j) -> p m j t", t=PACK, j=PACK)
-            src = wr.rearrange("p j (m t) -> p m j t", t=PACK)
-            cut = 64 if e % 4 == 3 else 0
-            if cut:
-                nc.vector.tensor_copy(dst[:, 0:cut], src[:, 0:cut])
-            nc.scalar.copy(dst[:, cut:P], src[:, cut:P])
+            wt = work.tile([P, H * PACK], BF16, name="wb", bufs=4, align_bytes=64)
+            wb[u] = wt
+            pack(u, cut(u), P, nc.scalar.copy)
+
+        def pack_vector(u):
+            if cut(u):
+                pack(u, 0, cut(u), nc.vector.tensor_copy)
+
+        def quant(u):
             wc = work.tile([P, H], U32, name="wc", bufs=3, align_bytes=64)
             ws = work.tile([P, H], U8, name="ws", bufs=3, align_bytes=64)
-            nc.vector.quantize_mx(out=wc[:].bitcast(FP8X4), scales=ws[:], in_=wb[:])
-            w2_q[e] = (wc, ws)
+            nc.vector.quantize_mx(out=wc[:].bitcast(FP8X4), scales=ws[:], in_=wb.pop(u)[:])
+            w_q[u] = (wc, ws)
 
-        da_q = []
-        pair = {}
+        bank = {}
+        da_q = {}
 
-        def layer2(e):
-            g = max(i for i in range(len(GROUPS)) if group_start[i] <= e * C)
-            cols = slice(e * C - group_start[g], e * C - group_start[g] + C)
-            wc, ws = w2_q.pop(e)
-            dh = psum.tile([P, PACK, C], F32, name="dh", bufs=3)
-            for t in range(PACK):
+        def multiply(u):
+            wc, ws = w_q.pop(u)
+            bk = psum.tile([P, QUAD, C], F32, name="bank", bufs=6)
+            for t in range(QUAD):
+                if u < E:
+                    e = u
+                    mc, ms = g_q[e // QUAD]
+                    cols = slice(e % QUAD * C, e % QUAD * C + C)
+                else:
+                    e = (u - E) % (E // QUAD) * QUAD + t
+                    mc, ms = da_q[e // 2]
+                    cols = slice(e % 2 * C, e % 2 * C + C)
                 nc.tensor.matmul_mx(
-                    out=dh[:, t, :],
+                    out=bk[:, t, :],
                     lhsT=wc[:, t * P : (t + 1) * P].bitcast(FP8X4),
                     lhsT_scale=ws[:, t * P : (t + 1) * P],
-                    rhs=g_codes[g][:, cols].bitcast(FP8X4),
-                    rhs_scale=g_scales[g][:, cols],
+                    rhs=mc[:, cols].bitcast(FP8X4),
+                    rhs_scale=ms[:, cols],
                     start=True,
                     stop=True,
                 )
+            bank[u] = bk
+
+        db = {}
+
+        def make_da(e):
             if e % 2 == 0:
-                db = work.tile([P, 2 * C * PACK], BF16, name="db", align_bytes=64)
-                pair["db"] = db
-            db = pair["db"]
-            half = e % 2 * C
-            a0 = e * C % A_W
+                dt = work.tile([P, 2 * C * PACK], BF16, name="db", align_bytes=64)
+                db[e // 2] = dt
+            c0 = e % 2 * C
             nc.vector.scalar_tensor_tensor(
-                db[:, half * PACK : (half + C) * PACK].rearrange("p (n t) -> p n t", t=PACK),
-                raw["a", e * C // A_W][:, :, a0 : a0 + C].rearrange("p t n -> p n t"),
+                db[e // 2][:, c0 * PACK : (c0 + C) * PACK].rearrange("p (n t) -> p n t", t=PACK),
+                a_t[e // 2][:, :, c0 : c0 + C].rearrange("p t n -> p n t"),
                 0.0,
-                dh[:].rearrange("p t n -> p n t"),
+                bank.pop(e)[:].rearrange("p t n -> p n t"),
                 MAX,
                 MULT,
             )
-            if e % 2 == 1:
-                dc = held.tile([P, 2 * C], U32, name=f"dc{e}", align_bytes=64)
-                ds = held.tile([P, 2 * C], U8, name=f"ds{e}", align_bytes=64)
-                nc.vector.quantize_mx(out=dc[:].bitcast(FP8X4), scales=ds[:], in_=db[:])
-                da_q.append((dc, ds))
+
+        def quant_da(pair):
+            dc = held.tile([P, 2 * C], U32, name=f"dc{pair}", align_bytes=64)
+            ds = held.tile([P, 2 * C], U8, name=f"ds{pair}", align_bytes=64)
+            nc.vector.quantize_mx(out=dc[:].bitcast(FP8X4), scales=ds[:], in_=db.pop(pair)[:])
+            da_q[pair] = (dc, ds)
+
+        def store_dx(u):
+            q, quad = divmod(u - E, E // QUAD)
+            nc.scalar.activation(
+                dx[q][:, quad * QUAD * C : (quad + 1) * QUAD * C],
+                bank.pop(u)[:].rearrange("p s c -> p (s c)"),
+                COPY,
+                scale=2.0,
+            )
+
+        r1 = {}
+        r2 = {}
+
+        def first(q):
+            def step():
+                rt = work.tile([P, T], F32, name="r1")
+                nc.vector.tensor_copy(rt[:], dx[q][:].indirect(pos1_t[:]))
+                r1[q] = rt
+            return step
+
+        def second(q):
+            def step():
+                rt = work.tile([P, T], F32, name="r2")
+                nc.vector.tensor_copy(rt[:], dx[q][:].indirect(pos2_t[:]))
+                r2[q] = rt
+            return step
+
+        def finish(q):
+            def step():
+                rt = work.tile([P, T], F32, name="res")
+                nc.vector.tensor_tensor(rt[:], r1[q][:], r2[q][:], ADD)
+                nc.sync.dma_start(out[q * P : (q + 1) * P, :], rt[:])
+            return step
+
+        combine = {15: [first(0)], 16: [second(0)], 17: [finish(0)], 18: [first(1)], 19: [second(1)], 20: [finish(1)], 21: [first(2)], 22: [second(2)], 23: [finish(2)]}
 
         advance(6)
-        make_g(0)
-        make_w2(0)
-        first_of_group = {group_start[g] // C: g for g in range(1, len(GROUPS))}
-        for e in range(E):
+        for j in range(PACK):
+            gather(0, j)
+        pack_g(0)
+        pack_scalar(0)
+        pack_vector(0)
+        gather(1, 0)
+        gather(1, 1)
+        quant_g(0)
+        pack_scalar(1)
+        pack_vector(1)
+        quant(0)
+        for u in range(UNITS):
             advance(2)
-            if e + 1 in first_of_group:
-                make_g(first_of_group[e + 1])
-            if e + 1 < E:
-                make_w2(e + 1)
-            layer2(e)
-
-        dx = []
-        for kt in range(K // P):
-            d = held.tile([P, S], F32, name=f"dx{kt}")
-            dx.append(d)
-
-        def combine(kt, queue):
-            r1 = work.tile([P, T], F32, name="r1")
-            r2 = work.tile([P, T], F32, name="r2")
-            res = work.tile([P, T], F32, name="res")
-
-            def first():
-                nc.vector.tensor_copy(r1[:], dx[kt][:].indirect(pos1_t[:]))
-
-            def second():
-                nc.vector.tensor_copy(r2[:], dx[kt][:].indirect(pos2_t[:]))
-
-            def finish():
-                nc.gpsimd.tensor_tensor(res[:], r1[:], r2[:], ADD)
-                queue.dma_start(out[kt * P : (kt + 1) * P, :], res[:])
-
-            return [first, second, finish]
-
-        k0 = 0
-        pending = []
-        for width in W1_WIDTHS:
-            n = H // width
-            for e in range(0, E, n):
-                while ("w1", k0, e) not in raw:
-                    advance(1)
-                advance(1)
-                wr = raw.pop(("w1", k0, e))
-                wb = work.tile([P, H * PACK], BF16, name="wb", bufs=3, align_bytes=64)
-                dst = wb[:].rearrange("p (s c i j) -> p s c j i", s=n, i=4, j=PACK)
-                src = wr.rearrange("p s j (c i) -> p s c j i", i=4)
-                for s in range(n):
-                    if s % 2 == 1:
-                        nc.vector.tensor_copy(dst[:, s], src[:, s])
-                    else:
-                        nc.scalar.copy(dst[:, s], src[:, s])
-                wc = work.tile([P, H], U32, name="wc", bufs=3, align_bytes=64)
-                ws = work.tile([P, H], U8, name="ws", bufs=3, align_bytes=64)
-                nc.vector.quantize_mx(out=wc[:].bitcast(FP8X4), scales=ws[:], in_=wb[:])
-                bank = psum.tile([P, width // P, n, C], F32, name="bank", bufs=4)
-                for s in range(n):
-                    dc, ds = da_q[(e + s) // 2]
-                    cols = slice((e + s) % 2 * C, (e + s) % 2 * C + C)
-                    for b in range(width // P):
-                        w0 = s * width + b * P
-                        nc.tensor.matmul_mx(
-                            out=bank[:, b, s, :],
-                            lhsT=wc[:, w0 : w0 + P].bitcast(FP8X4),
-                            lhsT_scale=ws[:, w0 : w0 + P],
-                            rhs=dc[:, cols].bitcast(FP8X4),
-                            rhs_scale=ds[:, cols],
-                            start=True,
-                            stop=True,
-                        )
-                for b in range(width // P):
-                    nc.scalar.activation(
-                        dx[k0 // P + b][:, e * C : (e + n) * C].rearrange("p (s c) -> p s c", c=C),
-                        bank[:, b],
-                        COPY,
-                        scale=2.0,
-                    )
-                if pending:
-                    pending.pop(0)()
-            last = k0 + width == K
-            for b in range(width // P):
-                pending += combine(k0 // P + b, nc.sync if last else nc.gpsimd)
-            k0 += width
-        for step in pending:
-            step()
+            multiply(u)
+            if u == E:
+                quant_da(E // 2 - 1)
+            if u + 2 < UNITS:
+                pack_scalar(u + 2)
+            if u < E:
+                make_da(u)
+            else:
+                store_dx(u)
+            if u + 1 < UNITS:
+                quant(u + 1)
+            if u + 2 < UNITS:
+                pack_vector(u + 2)
+            if u < E:
+                if u % 2 == 0 and u > 0:
+                    quant_da(u // 2 - 1)
+                if u % 4 == 3 and u // 4 + 1 < GROUPS:
+                    quant_g(u // 4 + 1)
+                n = PACK + 2 + u
+                if n < GROUPS * PACK:
+                    gather(n // PACK, n % PACK)
+                    if n % PACK == PACK - 1:
+                        pack_g(n // PACK)
+            for step in combine.get(u, ()):
+                step()
+        q = K // P - 1
+        first(q)()
+        rt = work.tile([P, T], F32, name="r2")
+        st = work.tile([P, T], F32, name="res")
+        for half in range(2):
+            cols = slice(half * T // 2, (half + 1) * T // 2)
+            lst = pos2_t[:, half * T // 32 : (half + 1) * T // 32]
+            nc.vector.tensor_copy(rt[:, cols], dx[q][:].indirect(lst))
+            nc.vector.tensor_tensor(st[:, cols], r1[q][:, cols], rt[:, cols], ADD)
+            nc.sync.dma_start(out[q * P : (q + 1) * P, cols], st[:, cols])

@@ -24,8 +24,7 @@ PACK = 4
 G_W = 512
 A_W = 256
 GROUPS = S // G_W
-W2_V = (0,) * 8 + (32,) * 4
-W1_V = (48,) * 6 + (32,) * 6
+VECTOR_PACKS = (5, 10, 13, 15, 17, 20)
 QUAD = 4
 UNITS = 2 * E
 
@@ -63,7 +62,6 @@ def tile_moe_bdx_mlp_relu2_kernel(tc, dyT, a, w2, w1, gate, offs, pos1, pos2, ou
         dy = []
         for j in range(PACK):
             d = held.tile([P, T], F32, name=f"dy{j}")
-            nc.sync.dma_start(d[:], dy_rows[:, j, :])
             dy.append(d)
 
         a_rows = a.rearrange("(p j) s -> p j s", j=PACK)
@@ -71,12 +69,12 @@ def tile_moe_bdx_mlp_relu2_kernel(tc, dyT, a, w2, w1, gate, offs, pos1, pos2, ou
         a_t = {}
 
         def load_a(g):
-            at = work.tile([P, PACK, A_W], F32, name="a_t", bufs=3)
+            at = work.tile([P, PACK, A_W], F32, name="a_t", bufs=4)
             nc.sync.dma_start(at[:], a_rows[:, :, g * A_W : (g + 1) * A_W])
             a_t[g] = at
 
         def load_unit(u):
-            wr = work.tile([P, PACK, H], F32, name="raw", bufs=9)
+            wr = work.tile([P, PACK, H], F32, name="raw", bufs=10)
             if u < E:
                 rows = w2[u].rearrange("(p j) i -> p j i", j=PACK)
                 for j in range(0, PACK, 2):
@@ -92,13 +90,18 @@ def tile_moe_bdx_mlp_relu2_kernel(tc, dyT, a, w2, w1, gate, offs, pos1, pos2, ou
             nc.sync.dma_start(pos1_t[:], pos1)
             nc.sync.dma_start(pos2_t[:], pos2)
 
+        for j in range(PACK):
+            if j == 2:
+                load_unit(0)
+            nc.sync.dma_start(dy[j][:], dy_rows[:, j, :])
         loads = []
         for u in range(UNITS):
-            loads.append(lambda u=u: load_unit(u))
+            if u > 0:
+                loads.append(lambda u=u: load_unit(u))
             if u < E and u % 2 == 0:
                 loads.append(lambda u=u: load_a(u // 2))
-                if u in (0, 4):
-                    loads.append(lambda u=u: load_gate(u // 4 + 1))
+            if u < 2:
+                loads.append(lambda u=u: load_gate(u + 1))
             if u == 10:
                 loads.append(load_pos)
 
@@ -117,15 +120,15 @@ def tile_moe_bdx_mlp_relu2_kernel(tc, dyT, a, w2, w1, gate, offs, pos1, pos2, ou
             lst = offs_t[:, g * G_W // 16 : (g + 1) * G_W // 16]
             nc.vector.tensor_tensor(g32[g][:, j, :], dy[j][:].indirect(lst), gate_t[g][:], MULT)
 
-        def interleave(dst, src, c0, c1, copy):
+        def interleave(dst, src, copy):
             copy(
-                dst[:].rearrange("p (c i j) -> p c j i", i=4, j=PACK)[:, c0:c1],
-                src[:].rearrange("p j (c i) -> p c j i", i=4)[:, c0:c1],
+                dst[:].rearrange("p (c i j) -> p c j i", i=4, j=PACK),
+                src[:].rearrange("p j (c i) -> p c j i", i=4),
             )
 
         def pack_g(g):
             gt = work.tile([P, G_W * PACK], BF16, name="gb", align_bytes=64)
-            interleave(gt, g32.pop(g), 0, G_W // 4, nc.scalar.copy)
+            interleave(gt, g32.pop(g), nc.scalar.copy)
             gb[g] = gt
 
         def quant_g(g):
@@ -134,28 +137,26 @@ def tile_moe_bdx_mlp_relu2_kernel(tc, dyT, a, w2, w1, gate, offs, pos1, pos2, ou
         wb = {}
         w_q = {}
 
-        def pack(u, c0, c1, copy):
-            if u < E:
-                copy(
-                    wb[u][:].rearrange("p (t m j) -> p m j t", t=PACK, j=PACK)[:, c0:c1],
-                    raw[u][:].rearrange("p j (m t) -> p m j t", t=PACK)[:, c0:c1],
-                )
-            else:
-                interleave(wb[u], raw[u], c0, c1, copy)
-
-        def cut(u):
-            return W2_V[u] if u < E else W1_V[u - E]
-
-        def pack_scalar(u):
+        def pack(u, copy):
             while u not in raw:
                 advance(1)
-            wt = work.tile([P, H * PACK], BF16, name="wb", bufs=4, align_bytes=64)
+            wt = work.tile([P, H * PACK], BF16, name="wb", bufs=5, align_bytes=64)
+            if u < E:
+                copy(
+                    wt[:].rearrange("p (t m j) -> p m j t", t=PACK, j=PACK),
+                    raw[u][:].rearrange("p j (m t) -> p m j t", t=PACK),
+                )
+            else:
+                interleave(wt, raw[u], copy)
             wb[u] = wt
-            pack(u, cut(u), P, nc.scalar.copy)
+
+        def pack_scalar(u):
+            if u not in VECTOR_PACKS:
+                pack(u, nc.scalar.copy)
 
         def pack_vector(u):
-            if cut(u):
-                pack(u, 0, cut(u), nc.vector.tensor_copy)
+            if u in VECTOR_PACKS:
+                pack(u, nc.vector.tensor_copy)
 
         def quant(u):
             wc = work.tile([P, H], U32, name="wc", bufs=3, align_bytes=64)
@@ -244,45 +245,49 @@ def tile_moe_bdx_mlp_relu2_kernel(tc, dyT, a, w2, w1, gate, offs, pos1, pos2, ou
                 nc.sync.dma_start(out[q * P : (q + 1) * P, :], rt[:])
             return step
 
-        combine = {15: [first(0)], 16: [second(0)], 17: [finish(0)], 18: [first(1)], 19: [second(1)], 20: [finish(1)], 21: [first(2)], 22: [second(2)], 23: [finish(2)]}
+        combine = {16: [first(0)], 17: [second(0)], 18: [finish(0)], 19: [first(1)], 20: [second(1)], 21: [finish(1)], 22: [first(2)], 23: [second(2)], 24: [finish(2)]}
 
         advance(6)
         for j in range(PACK):
             gather(0, j)
-        pack_g(0)
         pack_scalar(0)
         pack_vector(0)
+        pack_g(0)
         gather(1, 0)
         gather(1, 1)
         quant_g(0)
+        gather(1, 2)
+        gather(1, 3)
         pack_scalar(1)
         pack_vector(1)
         quant(0)
-        for u in range(UNITS):
-            advance(2)
-            multiply(u)
-            if u == E:
-                quant_da(E // 2 - 1)
-            if u + 2 < UNITS:
-                pack_scalar(u + 2)
-            if u < E:
-                make_da(u)
-            else:
-                store_dx(u)
+        pack_scalar(2)
+        for u in range(UNITS + 1):
+            if u < UNITS:
+                advance(2)
+                multiply(u)
+            if u - 1 >= E:
+                store_dx(u - 1)
+            if u + 3 < UNITS:
+                pack_scalar(u + 3)
+            if u == 1:
+                pack_g(1)
+            if u == 4:
+                pack_g(2)
             if u + 1 < UNITS:
                 quant(u + 1)
+            if u < PACK:
+                gather(2, u)
+            if 0 < u <= E:
+                make_da(u - 1)
             if u + 2 < UNITS:
                 pack_vector(u + 2)
-            if u < E:
-                if u % 2 == 0 and u > 0:
-                    quant_da(u // 2 - 1)
-                if u % 4 == 3 and u // 4 + 1 < GROUPS:
-                    quant_g(u // 4 + 1)
-                n = PACK + 2 + u
-                if n < GROUPS * PACK:
-                    gather(n // PACK, n % PACK)
-                    if n % PACK == PACK - 1:
-                        pack_g(n // PACK)
+            if u == 2:
+                quant_g(1)
+            if u == 6:
+                quant_g(2)
+            if u % 2 == 1 and 3 <= u <= E + 1:
+                quant_da((u - 3) // 2)
             for step in combine.get(u, ()):
                 step()
         q = K // P - 1

@@ -24,7 +24,7 @@ PACK = 4
 G_W = 512
 A_W = 256
 GROUPS = S // G_W
-VECTOR_PACKS = (5, 10, 13, 15, 17, 20)
+GPSIMD_COLS = 24
 QUAD = 4
 UNITS = 2 * E
 
@@ -47,10 +47,7 @@ def tile_moe_bdx_mlp_relu2_kernel(tc, dyT, a, w2, w1, gate, offs, pos1, pos2, ou
             gc = held.tile([P, G_W], U32, name=f"gc{g}", align_bytes=64)
             gs = held.tile([P, G_W], U8, name=f"gs{g}", align_bytes=64)
             g_q.append((gc, gs))
-        dx = []
-        for q in range(K // P):
-            d = held.tile([P, S], F32, name=f"dx{q}")
-            dx.append(d)
+        dx = {}
 
         nc.sync.dma_start(offs_t[:], offs)
 
@@ -61,7 +58,7 @@ def tile_moe_bdx_mlp_relu2_kernel(tc, dyT, a, w2, w1, gate, offs, pos1, pos2, ou
         dy_rows = dyT.rearrange("(p j) t -> p j t", j=PACK)
         dy = []
         for j in range(PACK):
-            d = held.tile([P, T], F32, name=f"dy{j}")
+            d = held.tile([P, T], F32, name=f"dy{j}", tag="plane", bufs=4)
             dy.append(d)
 
         a_rows = a.rearrange("(p j) s -> p j s", j=PACK)
@@ -69,12 +66,12 @@ def tile_moe_bdx_mlp_relu2_kernel(tc, dyT, a, w2, w1, gate, offs, pos1, pos2, ou
         a_t = {}
 
         def load_a(g):
-            at = work.tile([P, PACK, A_W], F32, name="a_t", bufs=4)
+            at = work.tile([P, PACK, A_W], F32, name="a_t", bufs=6)
             nc.sync.dma_start(at[:], a_rows[:, :, g * A_W : (g + 1) * A_W])
             a_t[g] = at
 
         def load_unit(u):
-            wr = work.tile([P, PACK, H], F32, name="raw", bufs=10)
+            wr = work.tile([P, PACK, H], F32, name="raw", bufs=12)
             if u < E:
                 rows = w2[u].rearrange("(p j) i -> p j i", j=PACK)
                 for j in range(0, PACK, 2):
@@ -91,17 +88,14 @@ def tile_moe_bdx_mlp_relu2_kernel(tc, dyT, a, w2, w1, gate, offs, pos1, pos2, ou
             nc.sync.dma_start(pos2_t[:], pos2)
 
         for j in range(PACK):
-            if j == 2:
-                load_unit(0)
             nc.sync.dma_start(dy[j][:], dy_rows[:, j, :])
         loads = []
         for u in range(UNITS):
-            if u > 0:
-                loads.append(lambda u=u: load_unit(u))
+            loads.append(lambda u=u: load_unit(u))
             if u < E and u % 2 == 0:
                 loads.append(lambda u=u: load_a(u // 2))
-            if u < 2:
-                loads.append(lambda u=u: load_gate(u + 1))
+            if u in (1, 3):
+                loads.append(lambda u=u: load_gate(u // 2 + 1))
             if u == 10:
                 loads.append(load_pos)
 
@@ -115,20 +109,20 @@ def tile_moe_bdx_mlp_relu2_kernel(tc, dyT, a, w2, w1, gate, offs, pos1, pos2, ou
 
         def gather(g, j):
             if j == 0:
-                gt = work.tile([P, PACK, G_W], F32, name="g32")
+                gt = work.tile([P, PACK, G_W], F32, name="g32", tag="g32")
                 g32[g] = gt
             lst = offs_t[:, g * G_W // 16 : (g + 1) * G_W // 16]
             nc.vector.tensor_tensor(g32[g][:, j, :], dy[j][:].indirect(lst), gate_t[g][:], MULT)
 
-        def interleave(dst, src, copy):
+        def interleave(dst, src, copy, c0=0, c1=H // 4):
             copy(
-                dst[:].rearrange("p (c i j) -> p c j i", i=4, j=PACK),
-                src[:].rearrange("p j (c i) -> p c j i", i=4),
+                dst[:].rearrange("p (c i j) -> p c j i", i=4, j=PACK)[:, c0:c1],
+                src[:].rearrange("p j (c i) -> p c j i", i=4)[:, c0:c1],
             )
 
         def pack_g(g):
-            gt = work.tile([P, G_W * PACK], BF16, name="gb", align_bytes=64)
-            interleave(gt, g32.pop(g), nc.scalar.copy)
+            gt = work.tile([P, G_W * PACK], BF16, name="gb", bufs=1, align_bytes=64)
+            interleave(gt, g32.pop(g), nc.vector.tensor_copy)
             gb[g] = gt
 
         def quant_g(g):
@@ -137,26 +131,22 @@ def tile_moe_bdx_mlp_relu2_kernel(tc, dyT, a, w2, w1, gate, offs, pos1, pos2, ou
         wb = {}
         w_q = {}
 
-        def pack(u, copy):
+        def gpsimd_copy(dst, src):
+            nc.gpsimd.tensor_scalar(dst, src, 1.0, 0.0, MULT, ADD)
+
+        def pack(u):
             while u not in raw:
                 advance(1)
             wt = work.tile([P, H * PACK], BF16, name="wb", bufs=5, align_bytes=64)
             if u < E:
-                copy(
+                nc.scalar.copy(
                     wt[:].rearrange("p (t m j) -> p m j t", t=PACK, j=PACK),
                     raw[u][:].rearrange("p j (m t) -> p m j t", t=PACK),
                 )
             else:
-                interleave(wt, raw[u], copy)
+                interleave(wt, raw[u], gpsimd_copy, c1=GPSIMD_COLS)
+                interleave(wt, raw[u], nc.scalar.copy, c0=GPSIMD_COLS)
             wb[u] = wt
-
-        def pack_scalar(u):
-            if u not in VECTOR_PACKS:
-                pack(u, nc.scalar.copy)
-
-        def pack_vector(u):
-            if u in VECTOR_PACKS:
-                pack(u, nc.vector.tensor_copy)
 
         def quant(u):
             wc = work.tile([P, H], U32, name="wc", bufs=3, align_bytes=64)
@@ -214,34 +204,31 @@ def tile_moe_bdx_mlp_relu2_kernel(tc, dyT, a, w2, w1, gate, offs, pos1, pos2, ou
 
         def store_dx(u):
             q, quad = divmod(u - E, E // QUAD)
-            nc.scalar.activation(
-                dx[q][:, quad * QUAD * C : (quad + 1) * QUAD * C],
-                bank.pop(u)[:].rearrange("p s c -> p (s c)"),
-                COPY,
-                scale=2.0,
-            )
+            if quad == 0:
+                d = held.tile([P, S], F32, name=f"dx{q}", tag="plane", bufs=4)
+                dx[q] = d
+            dst = dx[q][:, quad * QUAD * C : (quad + 1) * QUAD * C]
+            src = bank.pop(u)[:].rearrange("p s c -> p (s c)")
+            nc.scalar.activation(dst, src, COPY, scale=2.0)
 
-        r1 = {}
-        r2 = {}
+        picked = {}
 
         def first(q):
             def step():
-                rt = work.tile([P, T], F32, name="r1")
-                nc.vector.tensor_copy(rt[:], dx[q][:].indirect(pos1_t[:]))
-                r1[q] = rt
+                rt = work.tile([P, 2, T], F32, name="picked", tag="g32")
+                nc.vector.tensor_copy(rt[:, 0, :], dx[q][:].indirect(pos1_t[:]))
+                picked[q] = rt
             return step
 
         def second(q):
             def step():
-                rt = work.tile([P, T], F32, name="r2")
-                nc.vector.tensor_copy(rt[:], dx[q][:].indirect(pos2_t[:]))
-                r2[q] = rt
+                nc.vector.tensor_copy(picked[q][:, 1, :], dx[q][:].indirect(pos2_t[:]))
             return step
 
         def finish(q):
             def step():
                 rt = work.tile([P, T], F32, name="res")
-                nc.vector.tensor_tensor(rt[:], r1[q][:], r2[q][:], ADD)
+                nc.vector.tensor_tensor(rt[:], picked[q][:, 0, :], picked[q][:, 1, :], ADD)
                 nc.sync.dma_start(out[q * P : (q + 1) * P, :], rt[:])
             return step
 
@@ -250,18 +237,12 @@ def tile_moe_bdx_mlp_relu2_kernel(tc, dyT, a, w2, w1, gate, offs, pos1, pos2, ou
         advance(6)
         for j in range(PACK):
             gather(0, j)
-        pack_scalar(0)
-        pack_vector(0)
+        pack(0)
         pack_g(0)
-        gather(1, 0)
-        gather(1, 1)
         quant_g(0)
-        gather(1, 2)
-        gather(1, 3)
-        pack_scalar(1)
-        pack_vector(1)
         quant(0)
-        pack_scalar(2)
+        pack(1)
+        pack(2)
         for u in range(UNITS + 1):
             if u < UNITS:
                 advance(2)
@@ -269,34 +250,33 @@ def tile_moe_bdx_mlp_relu2_kernel(tc, dyT, a, w2, w1, gate, offs, pos1, pos2, ou
             if u - 1 >= E:
                 store_dx(u - 1)
             if u + 3 < UNITS:
-                pack_scalar(u + 3)
-            if u == 1:
-                pack_g(1)
-            if u == 4:
-                pack_g(2)
+                pack(u + 3)
             if u + 1 < UNITS:
                 quant(u + 1)
-            if u < PACK:
-                gather(2, u)
+            if u == 0:
+                for j in range(PACK):
+                    gather(1, j)
+                pack_g(1)
+            if u == 1:
+                quant_g(1)
+            if 2 <= u < 2 + PACK:
+                gather(2, u - 2)
+            if u == 1 + PACK:
+                pack_g(2)
+            if u == 2 + PACK:
+                quant_g(2)
             if 0 < u <= E:
                 make_da(u - 1)
-            if u + 2 < UNITS:
-                pack_vector(u + 2)
-            if u == 2:
-                quant_g(1)
-            if u == 6:
-                quant_g(2)
             if u % 2 == 1 and 3 <= u <= E + 1:
                 quant_da((u - 3) // 2)
             for step in combine.get(u, ()):
                 step()
         q = K // P - 1
         first(q)()
-        rt = work.tile([P, T], F32, name="r2")
         st = work.tile([P, T], F32, name="res")
         for half in range(2):
             cols = slice(half * T // 2, (half + 1) * T // 2)
             lst = pos2_t[:, half * T // 32 : (half + 1) * T // 32]
-            nc.vector.tensor_copy(rt[:, cols], dx[q][:].indirect(lst))
-            nc.vector.tensor_tensor(st[:, cols], r1[q][:, cols], rt[:, cols], ADD)
+            nc.vector.tensor_copy(picked[q][:, 1, cols], dx[q][:].indirect(lst))
+            nc.vector.tensor_tensor(st[:, cols], picked[q][:, 0, cols], picked[q][:, 1, cols], ADD)
             nc.sync.dma_start(out[q * P : (q + 1) * P, cols], st[:, cols])

from contextlib import ExitStack

import concourse.mybir as mybir

K, T, E, C, H, N = 512, 768, 12, 128, 512, 512
S = E * C

F32 = mybir.dt.float32
BF16 = mybir.dt.bfloat16
U32 = mybir.dt.uint32
U16 = mybir.dt.uint16
U8 = mybir.dt.uint8
FP8X4 = mybir.dt.float8_e4m3fn_x4
MULT = mybir.AluOpType.mult
ADD = mybir.AluOpType.add
MAX = mybir.AluOpType.max
COPY = mybir.ActivationFunctionType.Copy

FLOPS = 2 * 2 * S * N * H
BYTES = 4 * (N * T + H * S + 2 * E * N * H + S + K * T) + 2 * 128 * (S + 2 * T) // 16

P = 128
PACK = 4
G_W = 512
A_W = 256
GROUPS = S // G_W
GPSIMD_COLS = 24
QUAD = 4
UNITS = 2 * E


def tile_moe_bdx_mlp_relu2_kernel(tc, dyT, a, w2, w1, gate, offs, pos1, pos2, out):
    nc = tc.nc
    with ExitStack() as ctx:
        held = ctx.enter_context(tc.tile_pool(name="held", bufs=1))
        work = ctx.enter_context(tc.tile_pool(name="work", bufs=2))
        psum = ctx.enter_context(tc.psum_pool(name="psum", bufs=4))

        offs_t = held.tile([P, S // 16], U16)
        pos1_t = held.tile([P, T // 16], U16)
        pos2_t = held.tile([P, T // 16], U16)
        gate_t = []
        g_q = []
        for g in range(GROUPS):
            gt = held.tile([P, G_W], F32, name=f"gate{g}")
            gate_t.append(gt)
            gc = held.tile([P, G_W], U32, name=f"gc{g}", align_bytes=64)
            gs = held.tile([P, G_W], U8, name=f"gs{g}", align_bytes=64)
            g_q.append((gc, gs))
        dx = {}

        nc.sync.dma_start(offs_t[:], offs)

        def load_gate(g):
            nc.sync.dma_start(gate_t[g][:], gate[0:P, g * G_W : (g + 1) * G_W])

        load_gate(0)
        dy_rows = dyT.rearrange("(p j) t -> p j t", j=PACK)
        dy = []
        for j in range(PACK):
            d = held.tile([P, T], F32, name=f"dy{j}", tag="plane", bufs=4)
            dy.append(d)

        a_rows = a.rearrange("(p j) s -> p j s", j=PACK)
        raw = {}
        a_t = {}

        def load_a(g):
            at = work.tile([P, PACK, A_W], F32, name="a_t", bufs=6)
            nc.sync.dma_start(at[:], a_rows[:, :, g * A_W : (g + 1) * A_W])
            a_t[g] = at

        def load_unit(u):
            wr = work.tile([P, PACK, H], F32, name="raw", bufs=12)
            if u < E:
                rows = w2[u].rearrange("(p j) i -> p j i", j=PACK)
                for j in range(0, PACK, 2):
                    nc.sync.dma_start(wr[:, j : j + 2, :], rows[:, j : j + 2, :])
            else:
                q, quad = divmod(u - E, E // QUAD)
                for s in range(QUAD):
                    rows = w1[quad * QUAD + s].rearrange("(p j) k -> p j k", j=PACK)
                    nc.sync.dma_start(wr[:, :, s * P : (s + 1) * P], rows[:, :, q * P : (q + 1) * P])
            raw[u] = wr

        def load_pos():
            nc.sync.dma_start(pos1_t[:], pos1)
            nc.sync.dma_start(pos2_t[:], pos2)

        for j in range(PACK):
            nc.sync.dma_start(dy[j][:], dy_rows[:, j, :])
        loads = []
        for u in range(UNITS):
            loads.append(lambda u=u: load_unit(u))
            if u < E and u % 2 == 0:
                loads.append(lambda u=u: load_a(u // 2))
            if u in (1, 3):
                loads.append(lambda u=u: load_gate(u // 2 + 1))
            if u == 10:
                loads.append(load_pos)

        def advance(n):
            for _ in range(n):
                if loads:
                    loads.pop(0)()

        g32 = {}
        gb = {}

        def gather(g, j):
            if j == 0:
                gt = work.tile([P, PACK, G_W], F32, name="g32", tag="g32")
                g32[g] = gt
            lst = offs_t[:, g * G_W // 16 : (g + 1) * G_W // 16]
            nc.vector.tensor_tensor(g32[g][:, j, :], dy[j][:].indirect(lst), gate_t[g][:], MULT)

        def interleave(dst, src, copy, c0=0, c1=H // 4):
            copy(
                dst[:].rearrange("p (c i j) -> p c j i", i=4, j=PACK)[:, c0:c1],
                src[:].rearrange("p j (c i) -> p c j i", i=4)[:, c0:c1],
            )

        def pack_g(g):
            gt = work.tile([P, G_W * PACK], BF16, name="gb", bufs=1, align_bytes=64)
            interleave(gt, g32.pop(g), nc.vector.tensor_copy)
            gb[g] = gt

        def quant_g(g):
            nc.vector.quantize_mx(out=g_q[g][0][:].bitcast(FP8X4), scales=g_q[g][1][:], in_=gb.pop(g)[:])

        wb = {}
        w_q = {}

        def gpsimd_copy(dst, src):
            nc.gpsimd.tensor_scalar(dst, src, 1.0, 0.0, MULT, ADD)

        def pack(u):
            while u not in raw:
                advance(1)
            wt = work.tile([P, H * PACK], BF16, name="wb", bufs=5, align_bytes=64)
            if u < E:
                nc.scalar.copy(
                    wt[:].rearrange("p (t m j) -> p m j t", t=PACK, j=PACK),
                    raw[u][:].rearrange("p j (m t) -> p m j t", t=PACK),
                )
            else:
                interleave(wt, raw[u], gpsimd_copy, c1=GPSIMD_COLS)
                interleave(wt, raw[u], nc.scalar.copy, c0=GPSIMD_COLS)
            wb[u] = wt

        def quant(u):
            wc = work.tile([P, H], U32, name="wc", bufs=3, align_bytes=64)
            ws = work.tile([P, H], U8, name="ws", bufs=3, align_bytes=64)
            nc.vector.quantize_mx(out=wc[:].bitcast(FP8X4), scales=ws[:], in_=wb.pop(u)[:])
            w_q[u] = (wc, ws)

        bank = {}
        da_q = {}

        def multiply(u):
            wc, ws = w_q.pop(u)
            bk = psum.tile([P, QUAD, C], F32, name="bank", bufs=6)
            for t in range(QUAD):
                if u < E:
                    e = u
                    mc, ms = g_q[e // QUAD]
                    cols = slice(e % QUAD * C, e % QUAD * C + C)
                else:
                    e = (u - E) % (E // QUAD) * QUAD + t
                    mc, ms = da_q[e // 2]
                    cols = slice(e % 2 * C, e % 2 * C + C)
                nc.tensor.matmul_mx(
                    out=bk[:, t, :],
                    lhsT=wc[:, t * P : (t + 1) * P].bitcast(FP8X4),
                    lhsT_scale=ws[:, t * P : (t + 1) * P],
                    rhs=mc[:, cols].bitcast(FP8X4),
                    rhs_scale=ms[:, cols],
                    start=True,
                    stop=True,
                )
            bank[u] = bk

        db = {}

        def make_da(e):
            if e % 2 == 0:
                dt = work.tile([P, 2 * C * PACK], BF16, name="db", align_bytes=64)
                db[e // 2] = dt
            c0 = e % 2 * C
            nc.vector.scalar_tensor_tensor(
                db[e // 2][:, c0 * PACK : (c0 + C) * PACK].rearrange("p (n t) -> p n t", t=PACK),
                a_t[e // 2][:, :, c0 : c0 + C].rearrange("p t n -> p n t"),
                0.0,
                bank.pop(e)[:].rearrange("p t n -> p n t"),
                MAX,
                MULT,
            )

        def quant_da(pair):
            dc = held.tile([P, 2 * C], U32, name=f"dc{pair}", align_bytes=64)
            ds = held.tile([P, 2 * C], U8, name=f"ds{pair}", align_bytes=64)
            nc.vector.quantize_mx(out=dc[:].bitcast(FP8X4), scales=ds[:], in_=db.pop(pair)[:])
            da_q[pair] = (dc, ds)

        def store_dx(u):
            q, quad = divmod(u - E, E // QUAD)
            if quad == 0:
                d = held.tile([P, S], F32, name=f"dx{q}", tag="plane", bufs=4)
                dx[q] = d
            dst = dx[q][:, quad * QUAD * C : (quad + 1) * QUAD * C]
            src = bank.pop(u)[:].rearrange("p s c -> p (s c)")
            nc.scalar.activation(dst, src, COPY, scale=2.0)

        picked = {}

        def first(q):
            def step():
                rt = work.tile([P, 2, T], F32, name="picked", tag="g32")
                nc.vector.tensor_copy(rt[:, 0, :], dx[q][:].indirect(pos1_t[:]))
                picked[q] = rt
            return step

        def second(q):
            def step():
                nc.vector.tensor_copy(picked[q][:, 1, :], dx[q][:].indirect(pos2_t[:]))
            return step

        def finish(q):
            def step():
                rt = work.tile([P, T], F32, name="res")
                nc.vector.tensor_tensor(rt[:], picked[q][:, 0, :], picked[q][:, 1, :], ADD)
                nc.sync.dma_start(out[q * P : (q + 1) * P, :], rt[:])
            return step

        combine = {16: [first(0)], 17: [second(0)], 18: [finish(0)], 19: [first(1)], 20: [second(1)], 21: [finish(1)], 22: [first(2)], 23: [second(2)], 24: [finish(2)]}

        advance(6)
        for j in range(PACK):
            gather(0, j)
        pack(0)
        pack_g(0)
        quant_g(0)
        quant(0)
        pack(1)
        pack(2)
        for u in range(UNITS + 1):
            if u < UNITS:
                advance(2)
                multiply(u)
            if u - 1 >= E:
                store_dx(u - 1)
            if u + 3 < UNITS:
                pack(u + 3)
            if u + 1 < UNITS:
                quant(u + 1)
            if u == 0:
                for j in range(PACK):
                    gather(1, j)
                pack_g(1)
            if u == 1:
                quant_g(1)
            if 2 <= u < 2 + PACK:
                gather(2, u - 2)
            if u == 1 + PACK:
                pack_g(2)
            if u == 2 + PACK:
                quant_g(2)
            if 0 < u <= E:
                make_da(u - 1)
            if u % 2 == 1 and 3 <= u <= E + 1:
                quant_da((u - 3) // 2)
            for step in combine.get(u, ()):
                step()
        q = K // P - 1
        first(q)()
        st = work.tile([P, T], F32, name="res")
        for half in range(2):
            cols = slice(half * T // 2, (half + 1) * T // 2)
            lst = pos2_t[:, half * T // 32 : (half + 1) * T // 32]
            nc.vector.tensor_copy(picked[q][:, 1, cols], dx[q][:].indirect(lst))
            nc.vector.tensor_tensor(st[:, cols], picked[q][:, 0, cols], picked[q][:, 1, cols], ADD)
            nc.sync.dma_start(out[q * P : (q + 1) * P, cols], st[:, cols])
